import numpy as np
import ml_dtypes


def mxq(x, axis, fmt="e4m3"):
    dtype, down = {"e4m3": (ml_dtypes.float8_e4m3fn, 7), "e5m2": (ml_dtypes.float8_e5m2, 14)}[fmt]
    v = np.moveaxis(np.asarray(x, np.float32).astype(ml_dtypes.bfloat16).astype(np.float64), axis, -1)
    blocks = v.reshape(v.shape[:-1] + (-1, 32))
    amax = np.abs(blocks).max(-1, keepdims=True)
    byte = np.maximum(np.where(amax > 0, np.frexp(amax)[1] - 1 + 127, 0) - down, 1)
    scale = np.exp2(byte - 127.0)
    codes = (blocks / scale).astype(np.float32).astype(dtype).astype(np.float64)
    return np.moveaxis((codes * scale).reshape(v.shape), -1, axis)


WIDE = False


def mx_kscale(k):
    if not WIDE:
        return np.ones(k)
    levels = np.array([30, -30])
    if k % 512:
        return np.exp2(np.random.permutation(np.resize(levels, k // 32))).repeat(32)
    a = np.empty((k // 512, 16))
    for p in range(k // 512):
        a[p, :8] = np.random.permutation(np.resize(levels, 8))
        for g in range(8):
            far = levels[np.abs(levels - a[p, g]) >= 10]
            a[p, g + 8] = far[np.random.randint(len(far))]
    return np.exp2(a.ravel()).repeat(32)


def f64(x):
    return np.asarray(x).astype(np.float64)


def striped(idx):
    return np.tile(np.asarray(idx).reshape(-1, 16).T, (8, 1)).astype(np.uint16)


def unstriped(offs):
    return offs[:16].T.reshape(-1).astype(np.int64)


E2M1 = np.array([0.0, 0.5, 1.0, 1.5, 2.0, 3.0, 4.0, 6.0, -0.0, -0.5, -1.0, -1.5, -2.0, -3.0, -4.0, -6.0])


def pack_weight(w, fmt):
    k, n = w.shape
    w = f64(np.asarray(w, np.float32).astype(ml_dtypes.bfloat16)).reshape(k // 32, 32, n)
    amax = np.abs(w).max(1)
    if fmt in ("e4m3", "e5m2"):
        byte = np.frexp(amax)[1] - 1 + 127 - (7 if fmt == "e4m3" else 14)
    else:
        mant, ex = np.frexp(amax / 6.0)
        byte = np.where(mant > 0.5, ex, ex - 1) + 127
    byte = np.clip(np.where(amax > 0, byte, 1), 1, 254)
    scaled = (w * np.exp2(127.0 - byte)[:, None, :]).reshape(k, n).astype(np.float32)
    by_word = np.ascontiguousarray(scaled.reshape(k // 512, 128, 4, n).transpose(0, 1, 3, 2))
    if fmt in ("e4m3", "e5m2"):
        words = by_word.astype(ml_dtypes.float8_e4m3fn if fmt == "e4m3" else ml_dtypes.float8_e5m2).view(np.uint8)
    else:
        c = by_word.astype(ml_dtypes.float4_e2m1fn).view(np.uint8) & 0xF
        words = (c[..., 0::2] | (c[..., 1::2] << 4)).reshape(k // 512, 128, 2 * n)
    return np.ascontiguousarray(words), np.ascontiguousarray(byte.astype(np.uint8).reshape(k // 512, 16, n))


def unpack_weight(words, scales, fmt):
    g, _, n = scales.shape
    words = np.ascontiguousarray(words).reshape(g, 128, n, -1)
    if fmt in ("e4m3", "e5m2"):
        vals = words.view(ml_dtypes.float8_e4m3fn if fmt == "e4m3" else ml_dtypes.float8_e5m2).astype(np.float64)
    else:
        nib = np.empty((g, 128, n, 4), np.uint8)
        nib[..., 0::2] = words & 0xF
        nib[..., 1::2] = words >> 4
        vals = E2M1[nib]
    vals = vals * np.repeat(np.exp2(scales.astype(np.float64) - 127.0), 8, axis=1)[..., None]
    return vals.transpose(0, 1, 3, 2).reshape(g * 512, n)


def sigmoid(v):
    return 1.0 / (1.0 + np.exp(-v))


K, T, J, R, Q, N = 512, 1024, 256, 512, 1024, 256


def setup_inputs():
    n = np.random.standard_normal
    idx = np.random.permutation(T)[:J]
    idx2 = np.random.permutation(Q)[:J]
    fk = mx_kscale(K)
    fr = mx_kscale(R)
    xtp = pack_weight(n((K, T)) / fk[:, None], "e5m2")
    wp = pack_weight(n((K, R)) * 1 / np.sqrt(K) * fk[:, None] * fr, "e2m1")
    w2p = pack_weight(n((K, R)) * 1 / np.sqrt(K) * fk[:, None] * fr, "e4m3")
    wbp = pack_weight(n((R, N)) * 1 / np.sqrt(R) / fr[:, None], "e2m1")
    return {
        "xt_words": xtp[0],
        "xt_scales": xtp[1],
        "w_words": wp[0],
        "w_scales": wp[1],
        "w2_words": w2p[0],
        "w2_scales": w2p[1],
        "tg": (1.0 * n((R, Q))).astype(np.float32),
        "sg": (np.random.uniform(0.6, 1.6, (R, 1))).astype(np.float32),
        "bg": (np.random.uniform(-1.0, 1.0, (R, 1))).astype(np.float32),
        "wb_words": wbp[0],
        "wb_scales": wbp[1],
        "offs": striped(idx),
        "offs2": striped(idx2),
    }


def reference(xt_words, xt_scales, w_words, w_scales, w2_words, w2_scales, tg, sg, bg, wb_words, wb_scales, offs, offs2):
    idx = unstriped(offs)
    idx2 = unstriped(offs2)
    xtu = unpack_weight(xt_words, xt_scales, "e5m2")
    wu = unpack_weight(w_words, w_scales, "e2m1")
    w2u = unpack_weight(w2_words, w2_scales, "e4m3")
    wbu = unpack_weight(wb_words, wb_scales, "e2m1")
    xtidxg = xtu[:, idx]
    a = wu.T @ xtidxg
    b = w2u.T @ xtidxg
    hid = np.abs(a - b) * sigmoid(f64(tg)[:, idx2] * f64(sg) + f64(bg))
    hidq = mxq(hid, 0, "e4m3")
    y = wbu.T @ hidq
    return y

@@ -1,0 +1,177 @@
+from contextlib import ExitStack
+
+import concourse.mybir as mybir
+
+K, T, J, R, Q, N = 512, 1024, 256, 512, 1024, 256
+FLOPS = 2 * K * R * J * 2 + 2 * R * N * J
+
+F32 = mybir.dt.float32
+BF16 = mybir.dt.bfloat16
+I32 = mybir.dt.int32
+U32 = mybir.dt.uint32
+U16 = mybir.dt.uint16
+U8 = mybir.dt.uint8
+E4M3 = mybir.dt.float8_e4m3fn_x4
+E5M2 = mybir.dt.float8_e5m2_x4
+E2M1 = mybir.dt.float4_e2m1fn_x4
+ACT = mybir.ActivationFunctionType
+ALU = mybir.AluOpType
+
+P = 128
+PACK = 4
+
+
+def load_scale_rows(queue, plane, scales):
+    for quad in range(4):
+        queue.dma_start(
+            out=plane[32 * quad : 32 * quad + 4, :].bitcast(I32),
+            in_=scales[0, 4 * quad : 4 * quad + 4, :].bitcast(I32),
+        )
+
+
+def deal_columns(engine_copy, dealt, raw, run):
+    engine_copy(
+        out=dealt.rearrange("p (t c i) -> p c t i", t=PACK, i=run),
+        in_=raw.rearrange("p (c i t) -> p c t i", t=PACK, i=run),
+    )
+
+
+def tile_list_twow_tablegate_one_plain_kernel(
+    tc, xt_words, xt_scales, w_words, w_scales, w2_words, w2_scales, tg, sg, bg, wb_words, wb_scales, offs, offs2, out
+):
+    nc = tc.nc
+    with ExitStack() as ctx:
+        sb = ctx.enter_context(tc.tile_pool(name="sb", bufs=1))
+        psum = ctx.enter_context(tc.psum_pool(name="psum", bufs=1))
+
+        tokens = sb.tile([P, J // 16], U16, name="tokens")
+        entries = sb.tile([P, J // 16], U16, name="entries")
+        x_words = sb.tile([P, T], U32, name="x_words", align_bytes=64)
+        x_plane = sb.tile([P, T], U8, name="x_plane", align_bytes=64)
+        w_raw = sb.tile([P, R], U16, name="w_raw", align_bytes=64)
+        w2_raw = sb.tile([P, R], U32, name="w2_raw", align_bytes=64)
+        w_plane_raw = sb.tile([P, R], U8, name="w_plane_raw", align_bytes=64)
+        w2_plane_raw = sb.tile([P, R], U8, name="w2_plane_raw", align_bytes=64)
+        wb_codes = sb.tile([P, N], U16, name="wb_codes", align_bytes=64)
+        wb_plane = sb.tile([P, N], U8, name="wb_plane", align_bytes=64)
+        slope = sb.tile([P, PACK], F32, name="slope")
+        offset = sb.tile([P, PACK], F32, name="offset")
+        table = [sb.tile([P, Q], F32, name=f"table{t}", align_bytes=64) for t in range(PACK)]
+
+        nc.gpsimd.memset(x_plane[:].bitcast(I32), 0)
+        nc.gpsimd.memset(w_plane_raw[:].bitcast(I32), 0)
+        nc.vector.memset(w2_plane_raw[:].bitcast(I32), 0)
+        nc.vector.memset(wb_plane[:].bitcast(I32), 0)
+
+        tg_rows = tg.rearrange("(p t) q -> t p q", t=PACK)
+        nc.sync.dma_start(out=tokens[:], in_=offs)
+        nc.sync.dma_start(out=x_words[:].bitcast(I32), in_=xt_words[0].rearrange("p c t -> p (c t)").bitcast(I32))
+        load_scale_rows(nc.scalar, x_plane, xt_scales)
+        load_scale_rows(nc.gpsimd, w_plane_raw, w_scales)
+        nc.sync.dma_start(out=w2_raw[:].bitcast(I32), in_=w2_words[0].rearrange("p c t -> p (c t)").bitcast(I32))
+        nc.sync.dma_start(out=table[0][:], in_=tg_rows[0])
+        nc.sync.dma_start(out=w_raw[:].bitcast(I32), in_=w_words[0].bitcast(I32))
+        nc.sync.dma_start(out=table[1][:], in_=tg_rows[1])
+        load_scale_rows(nc.scalar, w2_plane_raw, w2_scales)
+        nc.gpsimd.dma_start(out=slope[:], in_=sg.rearrange("(p t) o -> p (t o)", t=PACK))
+        nc.gpsimd.dma_start(out=offset[:], in_=bg.rearrange("(p t) o -> p (t o)", t=PACK))
+        nc.sync.dma_start(out=entries[:], in_=offs2)
+        nc.sync.dma_start(out=table[2][:], in_=tg_rows[2])
+        nc.sync.dma_start(out=table[3][:], in_=tg_rows[3])
+        nc.sync.dma_start(out=wb_codes[:].bitcast(I32), in_=wb_words[0].bitcast(I32))
+        load_scale_rows(nc.sync, wb_plane, wb_scales)
+
+        xg_plane = sb.tile([P, J], U8, name="xg_plane", align_bytes=64)
+        xg_words = sb.tile([P, J], U32, name="xg_words", align_bytes=64)
+        nc.vector.tensor_copy(out=xg_plane[:], in_=x_plane[:].indirect(tokens[:]))
+        nc.vector.tensor_copy(out=xg_words[:], in_=x_words[:].indirect(tokens[:]))
+
+        w2_codes = sb.tile([P, R], U32, name="w2_codes", align_bytes=64)
+        w_codes = sb.tile([P, R], U16, name="w_codes", align_bytes=64)
+        w2_plane = sb.tile([P, R], U8, name="w2_plane", align_bytes=64)
+        w_plane = sb.tile([P, R], U8, name="w_plane", align_bytes=64)
+        deal_columns(nc.vector.tensor_copy, w2_codes[:], w2_raw[:], 4)
+        deal_columns(nc.vector.tensor_copy, w2_plane[:], w2_plane_raw[:], 16)
+        deal_columns(nc.vector.tensor_copy, w_codes[:], w_raw[:], 8)
+        deal_columns(nc.vector.tensor_copy, w_plane[:], w_plane_raw[:], 16)
+
+        a_ps = [psum.tile([P, 2, J], F32, name=f"a_ps{h}") for h in range(2)]
+        b_ps = [psum.tile([P, 2, J], F32, name=f"b_ps{h}") for h in range(2)]
+        for t in range(PACK):
+            cols = slice(P * t, P * (t + 1))
+            nc.tensor.matmul_mx(
+                out=b_ps[t // 2][:, t % 2, :],
+                lhsT=w2_codes[:, cols].bitcast(E4M3),
+                lhsT_scale=w2_plane[:, cols],
+                rhs=xg_words[:].bitcast(E5M2),
+                rhs_scale=xg_plane[:],
+                start=True,
+                stop=True,
+            )
+        for t in range(PACK):
+            cols = slice(P * t, P * (t + 1))
+            nc.tensor.matmul_mx(
+                out=a_ps[t // 2][:, t % 2, :],
+                lhsT=w_codes[:, cols].bitcast(E2M1),
+                lhsT_scale=w_plane[:, cols],
+                rhs=xg_words[:].bitcast(E5M2),
+                rhs_scale=xg_plane[:],
+                start=True,
+                stop=True,
+            )
+
+        gate = [sb.tile([P, J], F32, name=f"gate{t}") for t in range(PACK)]
+        b_sb = [sb.tile([P, 2, J], F32, name=f"b_sb{h}") for h in range(2)]
+        diff = [sb.tile([P, 2, J], F32, name=f"diff{h}") for h in range(2)]
+        size = [sb.tile([P, 2, J], F32, name=f"size{h}") for h in range(2)]
+        hid_rows = sb.tile([P, PACK, J], BF16, name="hid_rows", align_bytes=64)
+
+        def look(t):
+            nc.scalar.activation(
+                out=gate[t][:],
+                in_=table[t][:].indirect(entries[:]),
+                func=ACT.Sigmoid,
+                bias=offset[:, t : t + 1],
+                scale=slope[:, t : t + 1],
+            )
+
+        look(0)
+        for h in range(2):
+            nc.scalar.copy(out=b_sb[h][:], in_=b_ps[h][:])
+        look(1)
+        for h in range(2):
+            nc.vector.tensor_tensor(out=diff[h][:], in0=a_ps[h][:], in1=b_sb[h][:], op=ALU.subtract)
+            nc.scalar.activation(out=size[h][:], in_=diff[h][:], func=ACT.Abs)
+        look(2)
+        look(3)
+        for t in range(PACK):
+            nc.vector.tensor_tensor(out=hid_rows[:, t, :], in0=size[t // 2][:, t % 2, :], in1=gate[t][:], op=ALU.mult)
+
+        hid = sb.tile([P, J * PACK], BF16, name="hid", align_bytes=64)
+        nc.vector.tensor_copy(
+            out=hid[:].rearrange("p (c i t) -> p c t i", t=PACK, i=4),
+            in_=hid_rows[:].rearrange("p t (c i) -> p c t i", i=4),
+        )
+        hid_codes = sb.tile([P, J], U32, name="hid_codes", align_bytes=64)
+        hid_plane = sb.tile([P, J], U8, name="hid_plane", align_bytes=64)
+        nc.vector.quantize_mx(out=hid_codes[:].bitcast(E4M3), scales=hid_plane[:], in_=hid[:])
+
+        for c in range(N // P):
+            cols = slice(P * c, P * (c + 1))
+            y_ps = psum.tile([P, J], F32, name=f"y_ps{c}")
+            nc.tensor.matmul_mx(
+                out=y_ps[:],
+                lhsT=wb_codes[:, cols].bitcast(E2M1),
+                lhsT_scale=wb_plane[:, cols],
+                rhs=hid_codes[:].bitcast(E4M3),
+                rhs_scale=hid_plane[:],
+                start=True,
+                stop=True,
+            )
+            y = sb.tile([P, J], F32, name=f"y{c}")
+            if c == 0:
+                nc.scalar.copy(out=y[:], in_=y_ps[:])
+                nc.scalar.dma_start(out=out[cols, :], in_=y[:])
+            else:
+                nc.vector.tensor_copy(out=y[:], in_=y_ps[:])
+                nc.sync.dma_start(out=out[cols, :], in_=y[:])

@@ -59,23 +59,28 @@ def tile_list_twow_tablegate_one_plain_kernel(
         table = [sb.tile([P, Q], F32, name=f"table{t}", align_bytes=64) for t in range(PACK)]
 
         nc.gpsimd.memset(x_plane[:].bitcast(I32), 0)
-        nc.gpsimd.memset(w_plane_raw[:].bitcast(I32), 0)
         nc.vector.memset(w2_plane_raw[:].bitcast(I32), 0)
+        nc.vector.memset(w_plane_raw[:].bitcast(I32), 0)
         nc.vector.memset(wb_plane[:].bitcast(I32), 0)
+
+        warm_in = sb.tile([P, 1], F32, name="warm_in")
+        warm_out = sb.tile([P, 1], F32, name="warm_out")
+        nc.vector.memset(warm_in[:], 0.0)
+        nc.scalar.activation(out=warm_out[:], in_=warm_in[:], func=ACT.Sigmoid)
 
         tg_rows = tg.rearrange("(p t) q -> t p q", t=PACK)
         nc.sync.dma_start(out=tokens[:], in_=offs)
+        nc.sync.dma_start(out=entries[:], in_=offs2)
+        load_scale_rows(nc.sync, x_plane, xt_scales)
         nc.sync.dma_start(out=x_words[:].bitcast(I32), in_=xt_words[0].rearrange("p c t -> p (c t)").bitcast(I32))
-        load_scale_rows(nc.scalar, x_plane, xt_scales)
-        load_scale_rows(nc.gpsimd, w_plane_raw, w_scales)
         nc.sync.dma_start(out=w2_raw[:].bitcast(I32), in_=w2_words[0].rearrange("p c t -> p (c t)").bitcast(I32))
-        nc.sync.dma_start(out=table[0][:], in_=tg_rows[0])
-        nc.sync.dma_start(out=w_raw[:].bitcast(I32), in_=w_words[0].bitcast(I32))
-        nc.sync.dma_start(out=table[1][:], in_=tg_rows[1])
-        load_scale_rows(nc.scalar, w2_plane_raw, w2_scales)
         nc.gpsimd.dma_start(out=slope[:], in_=sg.rearrange("(p t) o -> p (t o)", t=PACK))
         nc.gpsimd.dma_start(out=offset[:], in_=bg.rearrange("(p t) o -> p (t o)", t=PACK))
-        nc.sync.dma_start(out=entries[:], in_=offs2)
+        load_scale_rows(nc.sync, w2_plane_raw, w2_scales)
+        nc.sync.dma_start(out=w_raw[:].bitcast(I32), in_=w_words[0].bitcast(I32))
+        nc.sync.dma_start(out=table[0][:], in_=tg_rows[0])
+        nc.sync.dma_start(out=table[1][:], in_=tg_rows[1])
+        load_scale_rows(nc.sync, w_plane_raw, w_scales)
         nc.sync.dma_start(out=table[2][:], in_=tg_rows[2])
         nc.sync.dma_start(out=table[3][:], in_=tg_rows[3])
         nc.sync.dma_start(out=wb_codes[:].bitcast(I32), in_=wb_words[0].bitcast(I32))
@@ -93,38 +98,36 @@ def tile_list_twow_tablegate_one_plain_kernel(
         deal_columns(nc.vector.tensor_copy, w2_codes[:], w2_raw[:], 4)
         deal_columns(nc.vector.tensor_copy, w2_plane[:], w2_plane_raw[:], 16)
         deal_columns(nc.vector.tensor_copy, w_codes[:], w_raw[:], 8)
-        deal_columns(nc.vector.tensor_copy, w_plane[:], w_plane_raw[:], 16)
 
-        a_ps = [psum.tile([P, 2, J], F32, name=f"a_ps{h}") for h in range(2)]
+        def first_stage(result, codes, fmt, plane, t):
+            cols = slice(P * t, P * (t + 1))
+            nc.tensor.matmul_mx(
+                out=result,
+                lhsT=codes[:, cols].bitcast(fmt),
+                lhsT_scale=plane[:, cols],
+                rhs=xg_words[:].bitcast(E5M2),
+                rhs_scale=xg_plane[:],
+                start=True,
+                stop=True,
+            )
+
         b_ps = [psum.tile([P, 2, J], F32, name=f"b_ps{h}") for h in range(2)]
-        for t in range(PACK):
-            cols = slice(P * t, P * (t + 1))
-            nc.tensor.matmul_mx(
-                out=b_ps[t // 2][:, t % 2, :],
-                lhsT=w2_codes[:, cols].bitcast(E4M3),
-                lhsT_scale=w2_plane[:, cols],
-                rhs=xg_words[:].bitcast(E5M2),
-                rhs_scale=xg_plane[:],
-                start=True,
-                stop=True,
-            )
-        for t in range(PACK):
-            cols = slice(P * t, P * (t + 1))
-            nc.tensor.matmul_mx(
-                out=a_ps[t // 2][:, t % 2, :],
-                lhsT=w_codes[:, cols].bitcast(E2M1),
-                lhsT_scale=w_plane[:, cols],
-                rhs=xg_words[:].bitcast(E5M2),
-                rhs_scale=xg_plane[:],
-                start=True,
-                stop=True,
-            )
-
-        gate = [sb.tile([P, J], F32, name=f"gate{t}") for t in range(PACK)]
         b_sb = [sb.tile([P, 2, J], F32, name=f"b_sb{h}") for h in range(2)]
-        diff = [sb.tile([P, 2, J], F32, name=f"diff{h}") for h in range(2)]
-        size = [sb.tile([P, 2, J], F32, name=f"size{h}") for h in range(2)]
-        hid_rows = sb.tile([P, PACK, J], BF16, name="hid_rows", align_bytes=64)
+        for t in range(PACK):
+            first_stage(b_ps[t // 2][:, t % 2, :], w2_codes, E4M3, w2_plane, t)
+        nc.vector.tensor_copy(out=b_sb[0][:], in_=b_ps[0][:])
+
+        a_ps = [psum.tile([P, J], F32, name=f"a_ps{t}", tag=f"a_ps{t}") for t in range(PACK)]
+        for t in range(PACK):
+            nc.vector.tensor_copy(
+                out=w_plane[:, P * t : P * (t + 1)], in_=w_plane_raw[:].rearrange("p (m t) -> p t m", t=PACK)[:, t, :]
+            )
+            first_stage(a_ps[t][:], w_codes, E2M1, w_plane, t)
+
+        half = J // 2
+        gate = [sb.tile([P, J], F32, name=f"gate{t}") for t in range(PACK)]
+        diff = [sb.tile([P, J], F32, name=f"diff{t}") for t in range(PACK)]
+        gated = sb.tile([P, PACK, J], BF16, name="gated", align_bytes=64)
 
         def look(t):
             nc.scalar.activation(
@@ -135,43 +138,51 @@ def tile_list_twow_tablegate_one_plain_kernel(
                 scale=slope[:, t : t + 1],
             )
 
+        def apply_gate(t, cols):
+            nc.vector.tensor_tensor(out=gated[:, t, cols], in0=diff[t][:, cols], in1=gate[t][:, cols], op=ALU.mult)
+
         look(0)
-        for h in range(2):
-            nc.scalar.copy(out=b_sb[h][:], in_=b_ps[h][:])
-        look(1)
-        for h in range(2):
-            nc.vector.tensor_tensor(out=diff[h][:], in0=a_ps[h][:], in1=b_sb[h][:], op=ALU.subtract)
-            nc.scalar.activation(out=size[h][:], in_=diff[h][:], func=ACT.Abs)
-        look(2)
-        look(3)
+        nc.scalar.copy(out=b_sb[1][:], in_=b_ps[1][:])
+        for t in range(1, PACK):
+            look(t)
         for t in range(PACK):
-            nc.vector.tensor_tensor(out=hid_rows[:, t, :], in0=size[t // 2][:, t % 2, :], in1=gate[t][:], op=ALU.mult)
+            nc.vector.tensor_tensor(out=diff[t][:], in0=a_ps[t][:], in1=b_sb[t // 2][:, t % 2, :], op=ALU.subtract)
+        halves = [slice(half * s, half * (s + 1)) for s in range(2)]
+        for t in range(PACK - 1):
+            apply_gate(t, slice(0, J))
+        for s in range(2):
+            apply_gate(PACK - 1, halves[s])
 
-        hid = sb.tile([P, J * PACK], BF16, name="hid", align_bytes=64)
-        nc.vector.tensor_copy(
-            out=hid[:].rearrange("p (c i t) -> p c t i", t=PACK, i=4),
-            in_=hid_rows[:].rearrange("p t (c i) -> p c t i", i=4),
+        hid = [sb.tile([P, half * PACK], BF16, name=f"hid{s}", align_bytes=64) for s in range(2)]
+        nc.scalar.activation(
+            out=hid[0][:].rearrange("p (c i t) -> p c t i", t=PACK, i=4),
+            in_=gated[:, :, halves[0]].rearrange("p t (c i) -> p c t i", i=4),
+            func=ACT.Abs,
         )
-        hid_codes = sb.tile([P, J], U32, name="hid_codes", align_bytes=64)
-        hid_plane = sb.tile([P, J], U8, name="hid_plane", align_bytes=64)
-        nc.vector.quantize_mx(out=hid_codes[:].bitcast(E4M3), scales=hid_plane[:], in_=hid[:])
+        rows = gated[:, :, halves[1]].rearrange("p t j -> p j t")
+        nc.vector.scalar_tensor_tensor(
+            out=hid[1][:].rearrange("p (j t) -> p j t", t=PACK), in0=rows, scalar=-1.0, in1=rows, op0=ALU.mult, op1=ALU.max
+        )
 
-        for c in range(N // P):
-            cols = slice(P * c, P * (c + 1))
-            y_ps = psum.tile([P, J], F32, name=f"y_ps{c}")
-            nc.tensor.matmul_mx(
-                out=y_ps[:],
-                lhsT=wb_codes[:, cols].bitcast(E2M1),
-                lhsT_scale=wb_plane[:, cols],
-                rhs=hid_codes[:].bitcast(E4M3),
-                rhs_scale=hid_plane[:],
-                start=True,
-                stop=True,
-            )
-            y = sb.tile([P, J], F32, name=f"y{c}")
-            if c == 0:
-                nc.scalar.copy(out=y[:], in_=y_ps[:])
-                nc.scalar.dma_start(out=out[cols, :], in_=y[:])
-            else:
-                nc.vector.tensor_copy(out=y[:], in_=y_ps[:])
-                nc.sync.dma_start(out=out[cols, :], in_=y[:])
+        for s in range(2):
+            hid_codes = sb.tile([P, half], U32, name=f"hid_codes{s}", align_bytes=64)
+            hid_plane = sb.tile([P, half], U8, name=f"hid_plane{s}", align_bytes=64)
+            nc.vector.quantize_mx(out=hid_codes[:].bitcast(E4M3), scales=hid_plane[:], in_=hid[s][:])
+            y = sb.tile([P, N // P, half], F32, name=f"y{s}")
+            for c in range(N // P):
+                cols = slice(P * c, P * (c + 1))
+                y_ps = psum.tile([P, half], F32, name=f"y_ps{s}{c}", tag=f"a_ps{2 * s + c}")
+                nc.tensor.matmul_mx(
+                    out=y_ps[:],
+                    lhsT=wb_codes[:, cols].bitcast(E2M1),
+                    lhsT_scale=wb_plane[:, cols],
+                    rhs=hid_codes[:].bitcast(E4M3),
+                    rhs_scale=hid_plane[:],
+                    start=True,
+                    stop=True,
+                )
+                if c == 0:
+                    nc.scalar.copy(out=y[:, c, :], in_=y_ps[:])
+                else:
+                    nc.vector.tensor_copy(out=y[:, c, :], in_=y_ps[:])
+            nc.sync.dma_start(out=out[:, halves[s]].rearrange("(c p) j -> p c j", p=P), in_=y[:])

from contextlib import ExitStack

import concourse.mybir as mybir

K, T, J, R, Q, N = 512, 1024, 256, 512, 1024, 256
FLOPS = 2 * K * R * J * 2 + 2 * R * N * J

F32 = mybir.dt.float32
BF16 = mybir.dt.bfloat16
I32 = mybir.dt.int32
U32 = mybir.dt.uint32
U16 = mybir.dt.uint16
U8 = mybir.dt.uint8
E4M3 = mybir.dt.float8_e4m3fn_x4
E5M2 = mybir.dt.float8_e5m2_x4
E2M1 = mybir.dt.float4_e2m1fn_x4
ACT = mybir.ActivationFunctionType
ALU = mybir.AluOpType

P = 128
PACK = 4


def load_scale_rows(queue, plane, scales):
    for quad in range(4):
        queue.dma_start(
            out=plane[32 * quad : 32 * quad + 4, :].bitcast(I32),
            in_=scales[0, 4 * quad : 4 * quad + 4, :].bitcast(I32),
        )


def deal_columns(engine_copy, dealt, raw, run):
    engine_copy(
        out=dealt.rearrange("p (t c i) -> p c t i", t=PACK, i=run),
        in_=raw.rearrange("p (c i t) -> p c t i", t=PACK, i=run),
    )


def tile_list_twow_tablegate_one_plain_kernel(
    tc, xt_words, xt_scales, w_words, w_scales, w2_words, w2_scales, tg, sg, bg, wb_words, wb_scales, offs, offs2, out
):
    nc = tc.nc
    with ExitStack() as ctx:
        sb = ctx.enter_context(tc.tile_pool(name="sb", bufs=1))
        psum = ctx.enter_context(tc.psum_pool(name="psum", bufs=1))

        tokens = sb.tile([P, J // 16], U16, name="tokens")
        entries = sb.tile([P, J // 16], U16, name="entries")
        x_words = sb.tile([P, T], U32, name="x_words", align_bytes=64)
        x_plane = sb.tile([P, T], U8, name="x_plane", align_bytes=64)
        w_raw = sb.tile([P, R], U16, name="w_raw", align_bytes=64)
        w2_raw = sb.tile([P, R], U32, name="w2_raw", align_bytes=64)
        w_plane_raw = sb.tile([P, R], U8, name="w_plane_raw", align_bytes=64)
        w2_plane_raw = sb.tile([P, R], U8, name="w2_plane_raw", align_bytes=64)
        wb_codes = sb.tile([P, N], U16, name="wb_codes", align_bytes=64)
        wb_plane = sb.tile([P, N], U8, name="wb_plane", align_bytes=64)
        slope = sb.tile([P, PACK], F32, name="slope")
        offset = sb.tile([P, PACK], F32, name="offset")
        table = [sb.tile([P, Q], F32, name=f"table{t}", align_bytes=64) for t in range(PACK)]

        nc.gpsimd.memset(x_plane[:].bitcast(I32), 0)
        nc.vector.memset(w2_plane_raw[:].bitcast(I32), 0)
        nc.vector.memset(w_plane_raw[:].bitcast(I32), 0)
        nc.vector.memset(wb_plane[:].bitcast(I32), 0)

        warm_in = sb.tile([P, 1], F32, name="warm_in")
        warm_out = sb.tile([P, 1], F32, name="warm_out")
        nc.vector.memset(warm_in[:], 0.0)
        nc.scalar.activation(out=warm_out[:], in_=warm_in[:], func=ACT.Sigmoid)

        tg_rows = tg.rearrange("(p t) q -> t p q", t=PACK)
        nc.sync.dma_start(out=tokens[:], in_=offs)
        nc.sync.dma_start(out=entries[:], in_=offs2)
        load_scale_rows(nc.sync, x_plane, xt_scales)
        nc.sync.dma_start(out=x_words[:].bitcast(I32), in_=xt_words[0].rearrange("p c t -> p (c t)").bitcast(I32))
        nc.sync.dma_start(out=w2_raw[:].bitcast(I32), in_=w2_words[0].rearrange("p c t -> p (c t)").bitcast(I32))
        nc.gpsimd.dma_start(out=slope[:], in_=sg.rearrange("(p t) o -> p (t o)", t=PACK))
        nc.gpsimd.dma_start(out=offset[:], in_=bg.rearrange("(p t) o -> p (t o)", t=PACK))
        load_scale_rows(nc.sync, w2_plane_raw, w2_scales)
        nc.sync.dma_start(out=w_raw[:].bitcast(I32), in_=w_words[0].bitcast(I32))
        nc.sync.dma_start(out=table[0][:], in_=tg_rows[0])
        nc.sync.dma_start(out=table[1][:], in_=tg_rows[1])
        load_scale_rows(nc.sync, w_plane_raw, w_scales)
        nc.sync.dma_start(out=table[2][:], in_=tg_rows[2])
        nc.sync.dma_start(out=table[3][:], in_=tg_rows[3])
        nc.sync.dma_start(out=wb_codes[:].bitcast(I32), in_=wb_words[0].bitcast(I32))
        load_scale_rows(nc.sync, wb_plane, wb_scales)

        xg_plane = sb.tile([P, J], U8, name="xg_plane", align_bytes=64)
        xg_words = sb.tile([P, J], U32, name="xg_words", align_bytes=64)
        nc.vector.tensor_copy(out=xg_plane[:], in_=x_plane[:].indirect(tokens[:]))
        nc.vector.tensor_copy(out=xg_words[:], in_=x_words[:].indirect(tokens[:]))

        w2_codes = sb.tile([P, R], U32, name="w2_codes", align_bytes=64)
        w_codes = sb.tile([P, R], U16, name="w_codes", align_bytes=64)
        w2_plane = sb.tile([P, R], U8, name="w2_plane", align_bytes=64)
        w_plane = sb.tile([P, R], U8, name="w_plane", align_bytes=64)
        deal_columns(nc.vector.tensor_copy, w2_codes[:], w2_raw[:], 4)
        deal_columns(nc.vector.tensor_copy, w2_plane[:], w2_plane_raw[:], 16)
        deal_columns(nc.vector.tensor_copy, w_codes[:], w_raw[:], 8)

        def first_stage(result, codes, fmt, plane, t):
            cols = slice(P * t, P * (t + 1))
            nc.tensor.matmul_mx(
                out=result,
                lhsT=codes[:, cols].bitcast(fmt),
                lhsT_scale=plane[:, cols],
                rhs=xg_words[:].bitcast(E5M2),
                rhs_scale=xg_plane[:],
                start=True,
                stop=True,
            )

        b_ps = [psum.tile([P, 2, J], F32, name=f"b_ps{h}") for h in range(2)]
        b_sb = [sb.tile([P, 2, J], F32, name=f"b_sb{h}") for h in range(2)]
        for t in range(PACK):
            first_stage(b_ps[t // 2][:, t % 2, :], w2_codes, E4M3, w2_plane, t)
        nc.vector.tensor_copy(out=b_sb[0][:], in_=b_ps[0][:])

        a_ps = [psum.tile([P, J], F32, name=f"a_ps{t}", tag=f"a_ps{t}") for t in range(PACK)]
        for t in range(PACK):
            nc.vector.tensor_copy(
                out=w_plane[:, P * t : P * (t + 1)], in_=w_plane_raw[:].rearrange("p (m t) -> p t m", t=PACK)[:, t, :]
            )
            first_stage(a_ps[t][:], w_codes, E2M1, w_plane, t)

        half = J // 2
        gate = [sb.tile([P, J], F32, name=f"gate{t}") for t in range(PACK)]
        diff = [sb.tile([P, J], F32, name=f"diff{t}") for t in range(PACK)]
        gated = sb.tile([P, PACK, J], BF16, name="gated", align_bytes=64)

        def look(t):
            nc.scalar.activation(
                out=gate[t][:],
                in_=table[t][:].indirect(entries[:]),
                func=ACT.Sigmoid,
                bias=offset[:, t : t + 1],
                scale=slope[:, t : t + 1],
            )

        def apply_gate(t, cols):
            nc.vector.tensor_tensor(out=gated[:, t, cols], in0=diff[t][:, cols], in1=gate[t][:, cols], op=ALU.mult)

        look(0)
        nc.scalar.copy(out=b_sb[1][:], in_=b_ps[1][:])
        for t in range(1, PACK):
            look(t)
        for t in range(PACK):
            nc.vector.tensor_tensor(out=diff[t][:], in0=a_ps[t][:], in1=b_sb[t // 2][:, t % 2, :], op=ALU.subtract)
        halves = [slice(half * s, half * (s + 1)) for s in range(2)]
        for t in range(PACK - 1):
            apply_gate(t, slice(0, J))
        for s in range(2):
            apply_gate(PACK - 1, halves[s])

        hid = [sb.tile([P, half * PACK], BF16, name=f"hid{s}", align_bytes=64) for s in range(2)]
        nc.scalar.activation(
            out=hid[0][:].rearrange("p (c i t) -> p c t i", t=PACK, i=4),
            in_=gated[:, :, halves[0]].rearrange("p t (c i) -> p c t i", i=4),
            func=ACT.Abs,
        )
        rows = gated[:, :, halves[1]].rearrange("p t j -> p j t")
        nc.vector.scalar_tensor_tensor(
            out=hid[1][:].rearrange("p (j t) -> p j t", t=PACK), in0=rows, scalar=-1.0, in1=rows, op0=ALU.mult, op1=ALU.max
        )

        for s in range(2):
            hid_codes = sb.tile([P, half], U32, name=f"hid_codes{s}", align_bytes=64)
            hid_plane = sb.tile([P, half], U8, name=f"hid_plane{s}", align_bytes=64)
            nc.vector.quantize_mx(out=hid_codes[:].bitcast(E4M3), scales=hid_plane[:], in_=hid[s][:])
            y = sb.tile([P, N // P, half], F32, name=f"y{s}")
            for c in range(N // P):
                cols = slice(P * c, P * (c + 1))
                y_ps = psum.tile([P, half], F32, name=f"y_ps{s}{c}", tag=f"a_ps{2 * s + c}")
                nc.tensor.matmul_mx(
                    out=y_ps[:],
                    lhsT=wb_codes[:, cols].bitcast(E2M1),
                    lhsT_scale=wb_plane[:, cols],
                    rhs=hid_codes[:].bitcast(E4M3),
                    rhs_scale=hid_plane[:],
                    start=True,
                    stop=True,
                )
                if c == 0:
                    nc.scalar.copy(out=y[:, c, :], in_=y_ps[:])
                else:
                    nc.vector.tensor_copy(out=y[:, c, :], in_=y_ps[:])
            nc.sync.dma_start(out=out[:, halves[s]].rearrange("(c p) j -> p c j", p=P), in_=y[:])
